import numpy as np
import ml_dtypes


def mxq(x, axis, fmt="e4m3"):
    dtype, down = {"e4m3": (ml_dtypes.float8_e4m3fn, 7), "e5m2": (ml_dtypes.float8_e5m2, 14)}[fmt]
    v = np.moveaxis(np.asarray(x, np.float32).astype(ml_dtypes.bfloat16).astype(np.float64), axis, -1)
    blocks = v.reshape(v.shape[:-1] + (-1, 32))
    amax = np.abs(blocks).max(-1, keepdims=True)
    byte = np.maximum(np.where(amax > 0, np.frexp(amax)[1] - 1 + 127, 0) - down, 1)
    scale = np.exp2(byte - 127.0)
    codes = (blocks / scale).astype(np.float32).astype(dtype).astype(np.float64)
    return np.moveaxis((codes * scale).reshape(v.shape), -1, axis)


WIDE = False


def mx_kscale(k):
    if not WIDE:
        return np.ones(k)
    levels = np.array([10, -10, 5, -5, 0])
    if k % 512:
        return np.exp2(np.random.permutation(np.resize(levels, k // 32))).repeat(32)
    a = np.empty((k // 512, 16))
    for p in range(k // 512):
        a[p, :8] = np.random.permutation(np.resize(levels, 8))
        for g in range(8):
            far = levels[np.abs(levels - a[p, g]) >= 10]
            a[p, g + 8] = far[np.random.randint(len(far))]
    return np.exp2(a.ravel()).repeat(32)


def f64(x):
    return np.asarray(x).astype(np.float64)


def striped(idx):
    return np.tile(idx.reshape(-1, 16).T, (8, 1)).astype(np.uint16)


def unstriped(offs):
    return offs[:16].T.reshape(-1).astype(np.int64)


def pack_weight(w):
    k, n = w.shape
    w = f64(np.asarray(w, np.float32).astype(ml_dtypes.bfloat16)).reshape(k // 32, 32, n)
    amax = np.abs(w).max(1)
    byte = np.clip(np.where(amax > 0, np.frexp(amax)[1] - 1 + 127 - 7, 1), 1, 254)
    scaled = (w * np.exp2(127.0 - byte)[:, None, :]).reshape(k, n).astype(np.float32)
    words = np.ascontiguousarray(scaled.reshape(k // 512, 128, 4, n).transpose(0, 1, 3, 2)).astype(ml_dtypes.float8_e4m3fn).view(np.uint8)
    return words, np.ascontiguousarray(byte.astype(np.uint8).reshape(k // 512, 16, n))


def unpack_weight(words, scales):
    g, p, n, _ = words.shape
    vals = np.ascontiguousarray(words).view(ml_dtypes.float8_e4m3fn).astype(np.float64) * np.repeat(np.exp2(scales.astype(np.float64) - 127.0), 8, axis=1)[..., None]
    return vals.transpose(0, 1, 3, 2).reshape(g * 512, n)


K, T, S, N, G = 512, 1024, 512, 128, 1024


def setup_inputs():
    n = np.random.standard_normal
    s = mx_kscale(K)[:, None]
    packed_xT = pack_weight(n((K, T)) * s)
    packed_eT = pack_weight(n((K, T)) * s)
    packed_dT = pack_weight(n((K, G)) * s)
    return {
        "x_words": packed_xT[0],
        "x_scales": packed_xT[1],
        "e_words": packed_eT[0],
        "e_scales": packed_eT[1],
        "d_words": packed_dT[0],
        "d_scales": packed_dT[1],
        "wr": (n((K, N)) / np.sqrt(K) / s).astype(np.float32),
        "wn": (n((K, N)) / np.sqrt(K) / s).astype(np.float32),
        "wt": (n((K, N)) / np.sqrt(K) / s).astype(np.float32),
        "offs": striped(np.random.permutation(T)[:S]),
        "tail": striped(np.random.permutation(T)[:S]),
        "rel": striped(np.random.permutation(G)[:S]),
    }


def reference(x_words, x_scales, e_words, e_scales, d_words, d_scales, wr, wn, wt, offs, tail, rel):
    xq = unpack_weight(x_words, x_scales)[:, unstriped(offs)]
    wrq = mxq(f64(wr), 0, "e4m3")
    e_tail = unpack_weight(e_words, e_scales)[:, unstriped(tail)]
    z = e_tail.T @ wrq
    df = (xq.T @ wrq) - z
    d_rel = unpack_weight(d_words, d_scales)[:, unstriped(rel)]
    wnq = mxq(f64(wn), 0, "e4m3")
    n0 = d_rel.T @ wnq
    n2 = (n0) ** 2
    nrm = n0 / (np.sqrt(n2.sum(axis=1, keepdims=True) + 0.1))
    dn = df * nrm
    al = dn.sum(axis=1, keepdims=True)
    wtq = mxq(f64(wt), 0, "e4m3")
    dd = df - (nrm * al) + 0.7 * (d_rel.T @ wtq)
    return (dd) ** 2

@@ -1,0 +1,144 @@
+import concourse.mybir as mybir
+
+K, T, S, N = 512, 1024, 512, 128
+FLOPS = 4 * 2 * K * S * N
+
+F32 = mybir.dt.float32
+BF16 = mybir.dt.bfloat16
+I32 = mybir.dt.int32
+U32 = mybir.dt.uint32
+U16 = mybir.dt.uint16
+U8 = mybir.dt.uint8
+FP8X4 = mybir.dt.float8_e4m3fn_x4
+ACT = mybir.ActivationFunctionType
+ALU = mybir.AluOpType
+
+P = 128
+PACK = 4
+BLOCKS = S // P
+HALF = S // 2
+
+
+def tile_picked_ytransh_sq_p_kernel(tc, x_words, x_scales, e_words, e_scales, d_words, d_scales, wr, wn, wt, offs, tail, rel, out):
+    nc = tc.nc
+    with tc.tile_pool(name="keep", bufs=1) as keep, tc.psum_pool(name="psum", bufs=1) as psum:
+
+        def load_list(name, src):
+            t = keep.tile([P, S // 16], U16, name=name)
+            nc.sync.dma_start(t[:], src)
+            return t
+
+        def load_words(name, src):
+            t = keep.tile([P, T], U32, name=name, align_bytes=64)
+            nc.sync.dma_start(t[:].bitcast(I32), src[0].rearrange("p n j -> p (n j)").bitcast(I32))
+            return t
+
+        def load_scales(name, src):
+            t = keep.tile([P, T], U8, name=name, align_bytes=64)
+            rows = src[0].bitcast(I32)
+            nc.vector.memset(t[:].bitcast(I32), 0)
+            for q in range(4):
+                nc.sync.dma_start(t[32 * q : 32 * q + 4, :].bitcast(I32), rows[4 * q : 4 * q + 4, :])
+            return t
+
+        def load_weight(name, src):
+            t = keep.tile([P, PACK, N], F32, name=name)
+            nc.sync.dma_start(t[:], src.rearrange("(p j) n -> p j n", j=PACK))
+            return t
+
+        rel_t = load_list("rel_t", rel)
+        ds_t = load_scales("ds_t", d_scales)
+        wn_raw = load_weight("wn_raw", wn)
+        dw_t = load_words("dw_t", d_words)
+        wt_raw = load_weight("wt_raw", wt)
+        offs_t = load_list("offs_t", offs)
+        xs_t = load_scales("xs_t", x_scales)
+        xw_t = load_words("xw_t", x_words)
+        tail_t = load_list("tail_t", tail)
+        es_t = load_scales("es_t", e_scales)
+        wr_raw = load_weight("late", wr)
+        ew_t = load_words("ew_t", e_words)
+
+        def gather(name, table, offsets, dtype):
+            t = keep.tile([P, 16 * offsets.shape[1]], dtype, name=name, align_bytes=64)
+            nc.vector.tensor_copy(t[:], table[:].indirect(offsets))
+            return t
+
+        def interleave(dst, raw, sign):
+            nc.scalar.activation(
+                dst.rearrange("p (c i t) -> p c t i", i=4, t=PACK),
+                raw[:].rearrange("p t (c i) -> p c t i", i=4),
+                ACT.Copy,
+                scale=sign,
+            )
+
+        def quantize(name, grouped, width):
+            codes = keep.tile([P, width], U32, name=name + "_codes", align_bytes=64)
+            scales = keep.tile([P, width], U8, name=name + "_scales", align_bytes=64)
+            nc.vector.quantize_mx(out=codes[:].bitcast(FP8X4), scales=scales[:], in_=grouped[:])
+            return codes, scales
+
+        def product(acc, words, scales, w_codes, w_scales, start, stop):
+            nc.tensor.matmul_mx(out=acc, lhsT=words.bitcast(FP8X4), lhsT_scale=scales, rhs=w_codes.bitcast(FP8X4), rhs_scale=w_scales, start=start, stop=stop)
+
+        def cols(b):
+            return slice(b * P, (b + 1) * P)
+
+        ds_g = gather("ds_g", ds_t, rel_t[:], U8)
+        wn_b = keep.tile([P, N * PACK], BF16, align_bytes=64)
+        interleave(wn_b[:], wn_raw, 1.0)
+        wn_c, wn_s = quantize("wn", wn_b, N)
+        dw_g = gather("dw_g", dw_t, rel_t[:], U32)
+        n0_ps = psum.tile([P, S], F32)
+        for b in range(BLOCKS):
+            product(n0_ps[:, cols(b)], dw_g[:, cols(b)], ds_g[:, cols(b)], wn_c[:], wn_s[:], True, True)
+        wt_b = keep.tile([P, N * PACK], BF16, align_bytes=64)
+        interleave(wt_b[:], wt_raw, 1.0)
+        xs_g = gather("xs_g", xs_t, offs_t[:], U8)
+        wt_c, wt_s = quantize("wt", wt_b, N)
+        tr_ps = psum.tile([P, S], F32)
+        for b in range(BLOCKS):
+            product(tr_ps[:, cols(b)], dw_g[:, cols(b)], ds_g[:, cols(b)], wt_c[:], wt_s[:], True, True)
+        sq = keep.tile([P, S], F32)
+        ssum = keep.tile([P, BLOCKS], F32)
+        for b in range(BLOCKS):
+            nc.scalar.activation(sq[:, cols(b)], n0_ps[:, cols(b)], ACT.Square, accum_out=ssum[:, b : b + 1])
+        n0 = keep.tile([P, S], F32)
+        nc.scalar.copy(n0[:], n0_ps[:])
+        xw_g = gather("xw_g", xw_t, offs_t[:], U32)
+        wr_b = keep.tile([P, 2 * N * PACK], BF16, align_bytes=64)
+        interleave(wr_b[:, : N * PACK], wr_raw, 1.0)
+        interleave(wr_b[:, N * PACK :], wr_raw, -1.0)
+        es_g = gather("es_g", es_t, tail_t[:], U8)
+        wr_c, wr_s = quantize("wr", wr_b, 2 * N)
+        late = keep.tile([P, S + BLOCKS], F32, name="late")
+        v = late[:, :S]
+        nden = late[:, S:]
+        nc.scalar.activation(nden, ssum[:], ACT.Copy, scale=-1.0, bias=-0.1)
+        nc.scalar.activation(v, tr_ps[:], ACT.Copy, scale=0.7)
+        nrinv = keep.tile([P, BLOCKS], F32)
+        nc.vector.reciprocal(nrinv[:], nden)
+
+        ew_g = [gather("ew_g%d" % h, ew_t, tail_t[:, 16 * h : 16 * (h + 1)], U32) for h in range(2)]
+        junk = keep.tile([P, S], F32)
+        coef = keep.tile([P, BLOCKS], F32)
+        u = keep.tile([P, S], F32)
+        dd = keep.tile([P, S], F32)
+        res = keep.tile([P, S], F32)
+        out_v = out.rearrange("(b p) m -> p b m", p=P)
+        for h in range(2):
+            df = psum.tile([P, HALF], F32, name="df%d" % h)
+            for i in range(2):
+                b = 2 * h + i
+                product(df[:, cols(i)], xw_g[:, cols(b)], xs_g[:, cols(b)], wr_c[:, :N], wr_s[:, :N], True, False)
+                product(df[:, cols(i)], ew_g[h][:, cols(i)], es_g[:, cols(b)], wr_c[:, N:], wr_s[:, N:], False, True)
+            half = slice(h * HALF, (h + 1) * HALF)
+            nc.vector.tensor_tensor(u[:, half], df[:], v[:, half], ALU.add)
+            for i in range(2):
+                b = 2 * h + i
+                nc.vector.scalar_tensor_tensor(junk[:, cols(b)], df[:, cols(i)], nrinv[:, b : b + 1], n0[:, cols(b)], ALU.mult, ALU.mult, accum_out=coef[:, b : b + 1])
+            for i in range(2):
+                b = 2 * h + i
+                nc.vector.scalar_tensor_tensor(dd[:, cols(b)], n0[:, cols(b)], coef[:, b : b + 1], u[:, cols(b)], ALU.mult, ALU.add)
+                nc.scalar.activation(res[:, cols(b)], dd[:, cols(b)], ACT.Square)
+            nc.sync.dma_start(out_v[:, 2 * h : 2 * h + 2, :], res[:, half].rearrange("p (b m) -> p b m", m=N))

@@ -33,7 +33,7 @@ def tile_picked_ytransh_sq_p_kernel(tc, x_words, x_scales, e_words, e_scales, d_
             nc.sync.dma_start(t[:].bitcast(I32), src[0].rearrange("p n j -> p (n j)").bitcast(I32))
             return t
 
-        def load_scales(name, src):
+        def load_scale_rows(name, src):
             t = keep.tile([P, T], U8, name=name, align_bytes=64)
             rows = src[0].bitcast(I32)
             nc.vector.memset(t[:].bitcast(I32), 0)
@@ -41,23 +41,36 @@ def tile_picked_ytransh_sq_p_kernel(tc, x_words, x_scales, e_words, e_scales, d_
                 nc.sync.dma_start(t[32 * q : 32 * q + 4, :].bitcast(I32), rows[4 * q : 4 * q + 4, :])
             return t
 
+        def load_scales(name, src):
+            t = keep.tile([P, T], U8, name=name, align_bytes=64)
+            rows = src[0].bitcast(I32)
+            for q in range(4):
+                queue = nc.sync if q < 2 else nc.scalar
+                queue.dma_start(t[32 * q : 32 * (q + 1), :].bitcast(I32), rows[4 * q : 4 * q + 4, :].partition_broadcast(8))
+            return t
+
         def load_weight(name, src):
-            t = keep.tile([P, PACK, N], F32, name=name)
+            t = keep.tile([P, PACK, N], F32, name=name, align_bytes=64)
             nc.sync.dma_start(t[:], src.rearrange("(p j) n -> p j n", j=PACK))
             return t
 
         rel_t = load_list("rel_t", rel)
         ds_t = load_scales("ds_t", d_scales)
-        wn_raw = load_weight("wn_raw", wn)
         dw_t = load_words("dw_t", d_words)
-        wt_raw = load_weight("wt_raw", wt)
+        wn_raw = load_weight("wn_raw", wn)
         offs_t = load_list("offs_t", offs)
-        xs_t = load_scales("xs_t", x_scales)
+        xs_t = load_scale_rows("xs_t", x_scales)
+        wt_raw = load_weight("wt_raw", wt)
         xw_t = load_words("xw_t", x_words)
         tail_t = load_list("tail_t", tail)
-        es_t = load_scales("es_t", e_scales)
-        wr_raw = load_weight("late", wr)
+        es_t = load_scale_rows("es_t", e_scales)
+        wr_raw = load_weight("ew_g1", wr)
         ew_t = load_words("ew_t", e_words)
+
+        one = keep.tile([P, 1], F32)
+        nc.gpsimd.memset(one[:], 1.0)
+        warm = keep.tile([P, 1], F32)
+        nc.scalar.activation(warm[:], one[:], ACT.Abs_reciprocal_sqrt)
 
         def gather(name, table, offsets, dtype):
             t = keep.tile([P, 16 * offsets.shape[1]], dtype, name=name, align_bytes=64)
@@ -85,60 +98,78 @@ def tile_picked_ytransh_sq_p_kernel(tc, x_words, x_scales, e_words, e_scales, d_
             return slice(b * P, (b + 1) * P)
 
         ds_g = gather("ds_g", ds_t, rel_t[:], U8)
+        dw_g = gather("dw_g", dw_t, rel_t[:], U32)
         wn_b = keep.tile([P, N * PACK], BF16, align_bytes=64)
         interleave(wn_b[:], wn_raw, 1.0)
         wn_c, wn_s = quantize("wn", wn_b, N)
-        dw_g = gather("dw_g", dw_t, rel_t[:], U32)
         n0_ps = psum.tile([P, S], F32)
         for b in range(BLOCKS):
             product(n0_ps[:, cols(b)], dw_g[:, cols(b)], ds_g[:, cols(b)], wn_c[:], wn_s[:], True, True)
+        xs_g = gather("xs_g", xs_t, offs_t[:], U8)
         wt_b = keep.tile([P, N * PACK], BF16, align_bytes=64)
         interleave(wt_b[:], wt_raw, 1.0)
-        xs_g = gather("xs_g", xs_t, offs_t[:], U8)
         wt_c, wt_s = quantize("wt", wt_b, N)
         tr_ps = psum.tile([P, S], F32)
         for b in range(BLOCKS):
             product(tr_ps[:, cols(b)], dw_g[:, cols(b)], ds_g[:, cols(b)], wt_c[:], wt_s[:], True, True)
-        sq = keep.tile([P, S], F32)
+        sq = keep.tile([P, S], F32, name="wt_raw", align_bytes=64)
         ssum = keep.tile([P, BLOCKS], F32)
         for b in range(BLOCKS):
             nc.scalar.activation(sq[:, cols(b)], n0_ps[:, cols(b)], ACT.Square, accum_out=ssum[:, b : b + 1])
-        n0 = keep.tile([P, S], F32)
-        nc.scalar.copy(n0[:], n0_ps[:])
+        den = keep.tile([P, BLOCKS], F32)
+        nc.scalar.activation(den[:], ssum[:], ACT.Copy, bias=0.1)
+        rinv = keep.tile([P, BLOCKS], F32)
+        nc.scalar.activation(rinv[:], den[:], ACT.Abs_reciprocal_sqrt)
         xw_g = gather("xw_g", xw_t, offs_t[:], U32)
-        wr_b = keep.tile([P, 2 * N * PACK], BF16, align_bytes=64)
-        interleave(wr_b[:, : N * PACK], wr_raw, 1.0)
-        interleave(wr_b[:, N * PACK :], wr_raw, -1.0)
         es_g = gather("es_g", es_t, tail_t[:], U8)
-        wr_c, wr_s = quantize("wr", wr_b, 2 * N)
-        late = keep.tile([P, S + BLOCKS], F32, name="late")
-        v = late[:, :S]
-        nden = late[:, S:]
-        nc.scalar.activation(nden, ssum[:], ACT.Copy, scale=-1.0, bias=-0.1)
-        nc.scalar.activation(v, tr_ps[:], ACT.Copy, scale=0.7)
-        nrinv = keep.tile([P, BLOCKS], F32)
-        nc.vector.reciprocal(nrinv[:], nden)
+        wr_b = keep.tile([P, N * PACK], BF16, align_bytes=64)
+        interleave(wr_b[:], wr_raw, 1.0)
+        nwr_b = keep.tile([P, N * PACK], BF16, align_bytes=64)
+        interleave(nwr_b[:], wr_raw, -1.0)
+        wr_c, wr_s = quantize("wr", wr_b, N)
+        df = [psum.tile([P, N], F32, name="df%d" % b) for b in range(BLOCKS)]
+        for b in range(BLOCKS):
+            product(df[b][:], xw_g[:, cols(b)], xs_g[:, cols(b)], wr_c[:], wr_s[:], True, False)
+        ew_g = [gather("ew_g0", ew_t, tail_t[:, :16], U32)]
+        nwr_c, nwr_s = quantize("nwr", nwr_b, N)
+        ew_g.append(gather("ew_g1", ew_t, tail_t[:, 16:], U32))
+        for b in range(BLOCKS):
+            product(df[b][:], ew_g[b // 2][:, cols(b % 2)], es_g[:, cols(b)], nwr_c[:], nwr_s[:], False, True)
+        n0 = keep.tile([P, S], F32, name="wr_b", align_bytes=64)
+        for b in range(BLOCKS):
+            nc.scalar.activation(n0[:, cols(b)], n0_ps[:, cols(b)], ACT.Copy, scale=rinv[:, b : b + 1])
 
-        ew_g = [gather("ew_g%d" % h, ew_t, tail_t[:, 16 * h : 16 * (h + 1)], U32) for h in range(2)]
         junk = keep.tile([P, S], F32)
         coef = keep.tile([P, BLOCKS], F32)
-        u = keep.tile([P, S], F32)
+        w = keep.tile([P, S], F32)
         dd = keep.tile([P, S], F32)
         res = keep.tile([P, S], F32)
         out_v = out.rearrange("(b p) m -> p b m", p=P)
-        for h in range(2):
-            df = psum.tile([P, HALF], F32, name="df%d" % h)
-            for i in range(2):
-                b = 2 * h + i
-                product(df[:, cols(i)], xw_g[:, cols(b)], xs_g[:, cols(b)], wr_c[:, :N], wr_s[:, :N], True, False)
-                product(df[:, cols(i)], ew_g[h][:, cols(i)], es_g[:, cols(b)], wr_c[:, N:], wr_s[:, N:], False, True)
-            half = slice(h * HALF, (h + 1) * HALF)
-            nc.vector.tensor_tensor(u[:, half], df[:], v[:, half], ALU.add)
-            for i in range(2):
-                b = 2 * h + i
-                nc.vector.scalar_tensor_tensor(junk[:, cols(b)], df[:, cols(i)], nrinv[:, b : b + 1], n0[:, cols(b)], ALU.mult, ALU.mult, accum_out=coef[:, b : b + 1])
-            for i in range(2):
-                b = 2 * h + i
-                nc.vector.scalar_tensor_tensor(dd[:, cols(b)], n0[:, cols(b)], coef[:, b : b + 1], u[:, cols(b)], ALU.mult, ALU.add)
-                nc.scalar.activation(res[:, cols(b)], dd[:, cols(b)], ACT.Square)
-            nc.sync.dma_start(out_v[:, 2 * h : 2 * h + 2, :], res[:, half].rearrange("p (b m) -> p b m", m=N))
+
+        def dot(b):
+            nc.vector.scalar_tensor_tensor(junk[:, cols(b)], df[b][:], -1.0, n0[:, cols(b)], ALU.mult, ALU.mult, accum_out=coef[:, b : b + 1])
+
+        def project(b):
+            nc.vector.scalar_tensor_tensor(w[:, cols(b)], n0[:, cols(b)], coef[:, b : b + 1], df[b][:], ALU.mult, ALU.add)
+
+        def finish(lo, hi):
+            span = slice(lo * P, hi * P)
+            nc.vector.scalar_tensor_tensor(dd[:, span], tr_ps[:, span], 0.7, w[:, span], ALU.mult, ALU.add)
+            nc.scalar.activation(res[:, span], dd[:, span], ACT.Square)
+
+        def store(lo, hi):
+            nc.sync.dma_start(out_v[:, lo:hi, :], res[:, lo * P : hi * P].rearrange("p (b m) -> p b m", m=N))
+
+        dot(0)
+        dot(1)
+        project(0)
+        project(1)
+        dot(2)
+        dot(3)
+        finish(0, 2)
+        store(0, 2)
+        project(2)
+        project(3)
+        finish(2, 3)
+        finish(3, 4)
+        store(2, 4)

@@ -130,16 +130,18 @@ def tile_picked_ytransh_sq_p_kernel(tc, x_words, x_scales, e_words, e_scales, d_
         df = [psum.tile([P, N], F32, name="df%d" % b) for b in range(BLOCKS)]
         for b in range(BLOCKS):
             product(df[b][:], xw_g[:, cols(b)], xs_g[:, cols(b)], wr_c[:], wr_s[:], True, False)
-        ew_g = [gather("ew_g0", ew_t, tail_t[:, :16], U32)]
+        ew_a = gather("ew_a", ew_t, tail_t[:, :8], U32)
         nwr_c, nwr_s = quantize("nwr", nwr_b, N)
-        ew_g.append(gather("ew_g1", ew_t, tail_t[:, 16:], U32))
+        ew_b = gather("ew_g1", ew_t, tail_t[:, 8:16], U32)
+        ew_c = gather("nwr_b", ew_t, tail_t[:, 16:], U32)
+        ew_blocks = [ew_a[:], ew_b[:], ew_c[:, :P], ew_c[:, P:]]
         for b in range(BLOCKS):
-            product(df[b][:], ew_g[b // 2][:, cols(b % 2)], es_g[:, cols(b)], nwr_c[:], nwr_s[:], False, True)
+            product(df[b][:], ew_blocks[b], es_g[:, cols(b)], nwr_c[:], nwr_s[:], False, True)
         n0 = keep.tile([P, S], F32, name="wr_b", align_bytes=64)
         for b in range(BLOCKS):
             nc.scalar.activation(n0[:, cols(b)], n0_ps[:, cols(b)], ACT.Copy, scale=rinv[:, b : b + 1])
 
-        junk = keep.tile([P, S], F32)
+        junk = keep.tile([P, HALF], F32)
         coef = keep.tile([P, BLOCKS], F32)
         w = keep.tile([P, S], F32)
         dd = keep.tile([P, S], F32)
@@ -147,7 +149,8 @@ def tile_picked_ytransh_sq_p_kernel(tc, x_words, x_scales, e_words, e_scales, d_
         out_v = out.rearrange("(b p) m -> p b m", p=P)
 
         def dot(b):
-            nc.vector.scalar_tensor_tensor(junk[:, cols(b)], df[b][:], -1.0, n0[:, cols(b)], ALU.mult, ALU.mult, accum_out=coef[:, b : b + 1])
+            products = junk[:, cols(b)] if b < 2 else n0[:, cols(b - 2)]
+            nc.vector.scalar_tensor_tensor(products, df[b][:], -1.0, n0[:, cols(b)], ALU.mult, ALU.mult, accum_out=coef[:, b : b + 1])
 
         def project(b):
             nc.vector.scalar_tensor_tensor(w[:, cols(b)], n0[:, cols(b)], coef[:, b : b + 1], df[b][:], ALU.mult, ALU.add)

import concourse.mybir as mybir

K, T, S, N = 512, 1024, 512, 128
FLOPS = 4 * 2 * K * S * N

F32 = mybir.dt.float32
BF16 = mybir.dt.bfloat16
I32 = mybir.dt.int32
U32 = mybir.dt.uint32
U16 = mybir.dt.uint16
U8 = mybir.dt.uint8
FP8X4 = mybir.dt.float8_e4m3fn_x4
ACT = mybir.ActivationFunctionType
ALU = mybir.AluOpType

P = 128
PACK = 4
BLOCKS = S // P
HALF = S // 2


def tile_picked_ytransh_sq_p_kernel(tc, x_words, x_scales, e_words, e_scales, d_words, d_scales, wr, wn, wt, offs, tail, rel, out):
    nc = tc.nc
    with tc.tile_pool(name="keep", bufs=1) as keep, tc.psum_pool(name="psum", bufs=1) as psum:

        def load_list(name, src):
            t = keep.tile([P, S // 16], U16, name=name)
            nc.sync.dma_start(t[:], src)
            return t

        def load_words(name, src):
            t = keep.tile([P, T], U32, name=name, align_bytes=64)
            nc.sync.dma_start(t[:].bitcast(I32), src[0].rearrange("p n j -> p (n j)").bitcast(I32))
            return t

        def load_scale_rows(name, src):
            t = keep.tile([P, T], U8, name=name, align_bytes=64)
            rows = src[0].bitcast(I32)
            nc.vector.memset(t[:].bitcast(I32), 0)
            for q in range(4):
                nc.sync.dma_start(t[32 * q : 32 * q + 4, :].bitcast(I32), rows[4 * q : 4 * q + 4, :])
            return t

        def load_scales(name, src):
            t = keep.tile([P, T], U8, name=name, align_bytes=64)
            rows = src[0].bitcast(I32)
            for q in range(4):
                queue = nc.sync if q < 2 else nc.scalar
                queue.dma_start(t[32 * q : 32 * (q + 1), :].bitcast(I32), rows[4 * q : 4 * q + 4, :].partition_broadcast(8))
            return t

        def load_weight(name, src):
            t = keep.tile([P, PACK, N], F32, name=name, align_bytes=64)
            nc.sync.dma_start(t[:], src.rearrange("(p j) n -> p j n", j=PACK))
            return t

        rel_t = load_list("rel_t", rel)
        ds_t = load_scales("ds_t", d_scales)
        dw_t = load_words("dw_t", d_words)
        wn_raw = load_weight("wn_raw", wn)
        offs_t = load_list("offs_t", offs)
        xs_t = load_scale_rows("xs_t", x_scales)
        wt_raw = load_weight("wt_raw", wt)
        xw_t = load_words("xw_t", x_words)
        tail_t = load_list("tail_t", tail)
        es_t = load_scale_rows("es_t", e_scales)
        wr_raw = load_weight("ew_g1", wr)
        ew_t = load_words("ew_t", e_words)

        one = keep.tile([P, 1], F32)
        nc.gpsimd.memset(one[:], 1.0)
        warm = keep.tile([P, 1], F32)
        nc.scalar.activation(warm[:], one[:], ACT.Abs_reciprocal_sqrt)

        def gather(name, table, offsets, dtype):
            t = keep.tile([P, 16 * offsets.shape[1]], dtype, name=name, align_bytes=64)
            nc.vector.tensor_copy(t[:], table[:].indirect(offsets))
            return t

        def interleave(dst, raw, sign):
            nc.scalar.activation(
                dst.rearrange("p (c i t) -> p c t i", i=4, t=PACK),
                raw[:].rearrange("p t (c i) -> p c t i", i=4),
                ACT.Copy,
                scale=sign,
            )

        def quantize(name, grouped, width):
            codes = keep.tile([P, width], U32, name=name + "_codes", align_bytes=64)
            scales = keep.tile([P, width], U8, name=name + "_scales", align_bytes=64)
            nc.vector.quantize_mx(out=codes[:].bitcast(FP8X4), scales=scales[:], in_=grouped[:])
            return codes, scales

        def product(acc, words, scales, w_codes, w_scales, start, stop):
            nc.tensor.matmul_mx(out=acc, lhsT=words.bitcast(FP8X4), lhsT_scale=scales, rhs=w_codes.bitcast(FP8X4), rhs_scale=w_scales, start=start, stop=stop)

        def cols(b):
            return slice(b * P, (b + 1) * P)

        ds_g = gather("ds_g", ds_t, rel_t[:], U8)
        dw_g = gather("dw_g", dw_t, rel_t[:], U32)
        wn_b = keep.tile([P, N * PACK], BF16, align_bytes=64)
        interleave(wn_b[:], wn_raw, 1.0)
        wn_c, wn_s = quantize("wn", wn_b, N)
        n0_ps = psum.tile([P, S], F32)
        for b in range(BLOCKS):
            product(n0_ps[:, cols(b)], dw_g[:, cols(b)], ds_g[:, cols(b)], wn_c[:], wn_s[:], True, True)
        xs_g = gather("xs_g", xs_t, offs_t[:], U8)
        wt_b = keep.tile([P, N * PACK], BF16, align_bytes=64)
        interleave(wt_b[:], wt_raw, 1.0)
        wt_c, wt_s = quantize("wt", wt_b, N)
        tr_ps = psum.tile([P, S], F32)
        for b in range(BLOCKS):
            product(tr_ps[:, cols(b)], dw_g[:, cols(b)], ds_g[:, cols(b)], wt_c[:], wt_s[:], True, True)
        sq = keep.tile([P, S], F32, name="wt_raw", align_bytes=64)
        ssum = keep.tile([P, BLOCKS], F32)
        for b in range(BLOCKS):
            nc.scalar.activation(sq[:, cols(b)], n0_ps[:, cols(b)], ACT.Square, accum_out=ssum[:, b : b + 1])
        den = keep.tile([P, BLOCKS], F32)
        nc.scalar.activation(den[:], ssum[:], ACT.Copy, bias=0.1)
        rinv = keep.tile([P, BLOCKS], F32)
        nc.scalar.activation(rinv[:], den[:], ACT.Abs_reciprocal_sqrt)
        xw_g = gather("xw_g", xw_t, offs_t[:], U32)
        es_g = gather("es_g", es_t, tail_t[:], U8)
        wr_b = keep.tile([P, N * PACK], BF16, align_bytes=64)
        interleave(wr_b[:], wr_raw, 1.0)
        nwr_b = keep.tile([P, N * PACK], BF16, align_bytes=64)
        interleave(nwr_b[:], wr_raw, -1.0)
        wr_c, wr_s = quantize("wr", wr_b, N)
        df = [psum.tile([P, N], F32, name="df%d" % b) for b in range(BLOCKS)]
        for b in range(BLOCKS):
            product(df[b][:], xw_g[:, cols(b)], xs_g[:, cols(b)], wr_c[:], wr_s[:], True, False)
        ew_a = gather("ew_a", ew_t, tail_t[:, :8], U32)
        nwr_c, nwr_s = quantize("nwr", nwr_b, N)
        ew_b = gather("ew_g1", ew_t, tail_t[:, 8:16], U32)
        ew_c = gather("nwr_b", ew_t, tail_t[:, 16:], U32)
        ew_blocks = [ew_a[:], ew_b[:], ew_c[:, :P], ew_c[:, P:]]
        for b in range(BLOCKS):
            product(df[b][:], ew_blocks[b], es_g[:, cols(b)], nwr_c[:], nwr_s[:], False, True)
        n0 = keep.tile([P, S], F32, name="wr_b", align_bytes=64)
        for b in range(BLOCKS):
            nc.scalar.activation(n0[:, cols(b)], n0_ps[:, cols(b)], ACT.Copy, scale=rinv[:, b : b + 1])

        junk = keep.tile([P, HALF], F32)
        coef = keep.tile([P, BLOCKS], F32)
        w = keep.tile([P, S], F32)
        dd = keep.tile([P, S], F32)
        res = keep.tile([P, S], F32)
        out_v = out.rearrange("(b p) m -> p b m", p=P)

        def dot(b):
            products = junk[:, cols(b)] if b < 2 else n0[:, cols(b - 2)]
            nc.vector.scalar_tensor_tensor(products, df[b][:], -1.0, n0[:, cols(b)], ALU.mult, ALU.mult, accum_out=coef[:, b : b + 1])

        def project(b):
            nc.vector.scalar_tensor_tensor(w[:, cols(b)], n0[:, cols(b)], coef[:, b : b + 1], df[b][:], ALU.mult, ALU.add)

        def finish(lo, hi):
            span = slice(lo * P, hi * P)
            nc.vector.scalar_tensor_tensor(dd[:, span], tr_ps[:, span], 0.7, w[:, span], ALU.mult, ALU.add)
            nc.scalar.activation(res[:, span], dd[:, span], ACT.Square)

        def store(lo, hi):
            nc.sync.dma_start(out_v[:, lo:hi, :], res[:, lo * P : hi * P].rearrange("p (b m) -> p b m", m=N))

        dot(0)
        dot(1)
        project(0)
        project(1)
        dot(2)
        dot(3)
        finish(0, 2)
        store(0, 2)
        project(2)
        project(3)
        finish(2, 3)
        finish(3, 4)
        store(2, 4)
